import numpy as np
import ml_dtypes


def mxq(x, axis, fmt="e4m3"):
    dtype, down = {"e4m3": (ml_dtypes.float8_e4m3fn, 7), "e5m2": (ml_dtypes.float8_e5m2, 14)}[fmt]
    v = np.moveaxis(np.asarray(x, np.float32).astype(ml_dtypes.bfloat16).astype(np.float64), axis, -1)
    blocks = v.reshape(v.shape[:-1] + (-1, 32))
    amax = np.abs(blocks).max(-1, keepdims=True)
    byte = np.maximum(np.where(amax > 0, np.frexp(amax)[1] - 1 + 127, 0) - down, 1)
    scale = np.exp2(byte - 127.0)
    codes = (blocks / scale).astype(np.float32).astype(dtype).astype(np.float64)
    return np.moveaxis((codes * scale).reshape(v.shape), -1, axis)


WIDE = False


def mx_kscale(k):
    if not WIDE:
        return np.ones(k)
    levels = np.array([30, -30])
    if k % 512:
        return np.exp2(np.random.permutation(np.resize(levels, k // 32))).repeat(32)
    a = np.empty((k // 512, 16))
    for p in range(k // 512):
        a[p, :8] = np.random.permutation(np.resize(levels, 8))
        for g in range(8):
            far = levels[np.abs(levels - a[p, g]) >= 10]
            a[p, g + 8] = far[np.random.randint(len(far))]
    return np.exp2(a.ravel()).repeat(32)


def f64(x):
    return np.asarray(x).astype(np.float64)


def striped(idx):
    return np.tile(np.asarray(idx).reshape(-1, 16).T, (8, 1)).astype(np.uint16)


def unstriped(offs):
    return offs[:16].T.reshape(-1).astype(np.int64)


E2M1 = np.array([0.0, 0.5, 1.0, 1.5, 2.0, 3.0, 4.0, 6.0, -0.0, -0.5, -1.0, -1.5, -2.0, -3.0, -4.0, -6.0])


def pack_weight(w, fmt):
    k, n = w.shape
    w = f64(np.asarray(w, np.float32).astype(ml_dtypes.bfloat16)).reshape(k // 32, 32, n)
    amax = np.abs(w).max(1)
    if fmt in ("e4m3", "e5m2"):
        byte = np.frexp(amax)[1] - 1 + 127 - (7 if fmt == "e4m3" else 14)
    else:
        mant, ex = np.frexp(amax / 6.0)
        byte = np.where(mant > 0.5, ex, ex - 1) + 127
    byte = np.clip(np.where(amax > 0, byte, 1), 1, 254)
    scaled = (w * np.exp2(127.0 - byte)[:, None, :]).reshape(k, n).astype(np.float32)
    by_word = np.ascontiguousarray(scaled.reshape(k // 512, 128, 4, n).transpose(0, 1, 3, 2))
    if fmt in ("e4m3", "e5m2"):
        words = by_word.astype(ml_dtypes.float8_e4m3fn if fmt == "e4m3" else ml_dtypes.float8_e5m2).view(np.uint8)
    else:
        c = by_word.astype(ml_dtypes.float4_e2m1fn).view(np.uint8) & 0xF
        words = (c[..., 0::2] | (c[..., 1::2] << 4)).reshape(k // 512, 128, 2 * n)
    return np.ascontiguousarray(words), np.ascontiguousarray(byte.astype(np.uint8).reshape(k // 512, 16, n))


def unpack_weight(words, scales, fmt):
    g, _, n = scales.shape
    words = np.ascontiguousarray(words).reshape(g, 128, n, -1)
    if fmt in ("e4m3", "e5m2"):
        vals = words.view(ml_dtypes.float8_e4m3fn if fmt == "e4m3" else ml_dtypes.float8_e5m2).astype(np.float64)
    else:
        nib = np.empty((g, 128, n, 4), np.uint8)
        nib[..., 0::2] = words & 0xF
        nib[..., 1::2] = words >> 4
        vals = E2M1[nib]
    vals = vals * np.repeat(np.exp2(scales.astype(np.float64) - 127.0), 8, axis=1)[..., None]
    return vals.transpose(0, 1, 3, 2).reshape(g * 512, n)


K, T, J, R, C, N, E = 512, 1024, 256, 512, 512, 256, 128


def setup_inputs():
    n = np.random.standard_normal
    idx = np.random.permutation(T)[:J]
    idx2 = np.random.permutation(C)[:J]
    idx3 = np.random.permutation(C)[:J]
    idx4 = np.random.permutation(J)[:E]
    idx5 = np.random.permutation(J)[:E]
    fk = mx_kscale(K)
    fr = mx_kscale(R)
    xtp = pack_weight(n((K, T)) / fk[:, None], "e5m2")
    wp = pack_weight(n((K, R)) * 1 / np.sqrt(K) * fk[:, None] * fr, "e2m1")
    w2p = pack_weight(n((K, R)) * 1 / np.sqrt(K) * fk[:, None] * fr, "e4m3")
    wbp = pack_weight(n((R, N)) * 1 / np.sqrt(R) / fr[:, None], "e2m1")
    wsp = pack_weight(n((K, N)) * 1 / np.sqrt(K) * fk[:, None], "e2m1")
    return {
        "xt_words": xtp[0],
        "xt_scales": xtp[1],
        "w_words": wp[0],
        "w_scales": wp[1],
        "w2_words": w2p[0],
        "w2_scales": w2p[1],
        "wb_words": wbp[0],
        "wb_scales": wbp[1],
        "ws_words": wsp[0],
        "ws_scales": wsp[1],
        "offs": striped(idx),
        "offs2": striped(idx2),
        "offs3": striped(idx3),
        "offs4": striped(idx4),
        "offs5": striped(idx5),
    }


def reference(xt_words, xt_scales, w_words, w_scales, w2_words, w2_scales, wb_words, wb_scales, ws_words, ws_scales, offs, offs2, offs3, offs4, offs5):
    idx = unstriped(offs)
    idx2 = unstriped(offs2)
    idx3 = unstriped(offs3)
    idx4 = unstriped(offs4)
    idx5 = unstriped(offs5)
    xtu = unpack_weight(xt_words, xt_scales, "e5m2")
    wu = unpack_weight(w_words, w_scales, "e2m1")
    w2u = unpack_weight(w2_words, w2_scales, "e4m3")
    wbu = unpack_weight(wb_words, wb_scales, "e2m1")
    wsu = unpack_weight(ws_words, ws_scales, "e2m1")
    xtidxg = xtu[:, idx]
    a = wu.T @ xtidxg
    b = w2u.T @ xtidxg
    pw = np.zeros((R, C))
    pw[:, idx2] = a
    hid = np.maximum(pw[:, idx3], b)
    hidq = mxq(hid, 0, "e4m3")
    p = wbu.T @ hidq + wsu.T @ xtidxg
    y = np.maximum(p[:, idx4], p[:, idx5])
    return y

@@ -1,0 +1,234 @@
+from contextlib import ExitStack
+
+import concourse.mybir as mybir
+
+K, T, J, R, C, N, E = 512, 1024, 256, 512, 512, 256, 128
+FLOPS = 2 * K * J * (R + R + N) + 2 * R * J * N
+
+F32 = mybir.dt.float32
+BF16 = mybir.dt.bfloat16
+I32 = mybir.dt.int32
+U32 = mybir.dt.uint32
+U16 = mybir.dt.uint16
+U8 = mybir.dt.uint8
+E4M3 = mybir.dt.float8_e4m3fn_x4
+E5M2 = mybir.dt.float8_e5m2_x4
+E2M1 = mybir.dt.float4_e2m1fn_x4
+COPY = mybir.ActivationFunctionType.Copy
+MAX = mybir.AluOpType.max
+
+P = 128
+PACK = 4
+HALF = J // 2
+
+
+def tile_list_twow_board_skip_bestoftwo_kernel(
+    tc, xt_words, xt_scales, w_words, w_scales, w2_words, w2_scales, wb_words, wb_scales,
+    ws_words, ws_scales, offs, offs2, offs3, offs4, offs5, out,
+):
+    nc = tc.nc
+    with ExitStack() as ctx:
+        lists = ctx.enter_context(tc.tile_pool(name="lists", bufs=1))
+        sb = ctx.enter_context(tc.tile_pool(name="sb", bufs=1))
+        psum = ctx.enter_context(tc.psum_pool(name="psum", bufs=1))
+
+        def list_tile(src, name):
+            tile = lists.tile(list(src.shape), U16, name=name)
+            nc.sync.dma_start(tile[:], src)
+            return tile
+
+        def load_scale_rows(queue, plane, src, q):
+            queue.dma_start(
+                out=plane[32 * q : 32 * q + 4, :].bitcast(I32),
+                in_=src[0, 4 * q : 4 * q + 4, :].bitcast(I32),
+            )
+
+        def zeroed_plane(width, name):
+            plane = sb.tile([P, width], U8, name=name, align_bytes=64)
+            nc.vector.memset(plane[:].bitcast(I32), 0)
+            return plane
+
+        def load_words(src, width, dtype, name):
+            tile = sb.tile([P, width], dtype, name=name, align_bytes=64)
+            nc.sync.dma_start(out=tile[:].bitcast(I32), in_=src.bitcast(I32))
+            return tile
+
+        xs = zeroed_plane(T, "xs")
+        wsc = zeroed_plane(R, "wsc")
+        later = zeroed_plane(R + 2 * N, "later")
+        w2sc = later[:, 0:R]
+        wssc = later[:, R : R + N]
+        wbsc = later[:, R + N : R + 2 * N]
+
+        l1 = list_tile(offs, "l1")
+        ww = load_words(w_words[0], 2 * R, U8, "ww")
+        xw = load_words(xt_words[0].rearrange("p n t -> p (n t)"), T, U32, "xw")
+        for q in range(4):
+            load_scale_rows(nc.scalar, xs, xt_scales, q)
+        load_scale_rows(nc.gpsimd, wsc, w_scales, 0)
+        for q in range(1, 4):
+            load_scale_rows(nc.sync, wsc, w_scales, q)
+        w2w = load_words(w2_words[0].rearrange("p n t -> p (n t)"), R, U32, "w2w")
+        l2 = list_tile(offs2, "l2")
+        for q in range(4):
+            load_scale_rows(nc.sync, w2sc, w2_scales, q)
+        l3 = list_tile(offs3, "l3")
+        wsw = load_words(ws_words[0], 2 * N, U8, "wsw")
+        for q in range(4):
+            load_scale_rows(nc.sync, wssc, ws_scales, q)
+        wbw = load_words(wb_words[0], 2 * N, U8, "wbw")
+        for q in range(4):
+            load_scale_rows(nc.sync, wbsc, wb_scales, q)
+        l4 = list_tile(offs4, "l4")
+        l5 = list_tile(offs5, "l5")
+
+        boards = []
+        for t in range(PACK):
+            board = sb.tile([P, C], F32, name="board%d" % t)
+            nc.gpsimd.memset(board[:], 0.0)
+            boards.append(board)
+
+        wwp = sb.tile([P, 2 * R], U8, align_bytes=64)
+        nc.vector.tensor_copy(
+            out=wwp[:].bitcast(U16).rearrange("p (t m) -> p m t", t=PACK),
+            in_=ww[:].bitcast(U16).rearrange("p (m t) -> p m t", t=PACK),
+        )
+        xsg = sb.tile([P, J], U8, align_bytes=64)
+        nc.vector.tensor_copy(out=xsg[:], in_=xs[:].indirect(l1[:]))
+        xg = sb.tile([P, J], U32, align_bytes=64)
+        nc.vector.tensor_copy(out=xg[:], in_=xw[:].indirect(l1[:]))
+
+        wscp = sb.tile([P, R], U8, align_bytes=64)
+        a_ps = []
+        for t in range(PACK):
+            nc.vector.tensor_copy(
+                out=wscp[:, P * t : P * (t + 1)],
+                in_=wsc[:].rearrange("p (m t) -> p t m", t=PACK)[:, t, :],
+            )
+            acc = psum.tile([P, J], F32, name="a%d" % t, tag="bank%d" % t)
+            nc.tensor.matmul_mx(
+                out=acc[:],
+                lhsT=wwp[:, 2 * P * t : 2 * P * (t + 1)].bitcast(E2M1),
+                lhsT_scale=wscp[:, P * t : P * (t + 1)],
+                rhs=xg[:].bitcast(E5M2),
+                rhs_scale=xsg[:],
+                start=True,
+                stop=True,
+            )
+            a_ps.append(acc)
+
+        a_sb = [sb.tile([P, J], F32, name="a_sb%d" % t) for t in range(PACK)]
+        for t in (0, 1):
+            nc.scalar.activation(out=a_sb[t][:], in_=a_ps[t][:], func=COPY)
+
+        w2wp = sb.tile([P, R], U32, align_bytes=64)
+        nc.vector.tensor_copy(
+            out=w2wp[:].rearrange("p (t m) -> p m t", t=PACK),
+            in_=w2w[:].rearrange("p (m t) -> p m t", t=PACK),
+        )
+        w2scp = sb.tile([P, R], U8, align_bytes=64)
+        nc.vector.tensor_copy(
+            out=w2scp[:].rearrange("p (t m) -> p t m", t=PACK),
+            in_=w2sc.rearrange("p (m t) -> p t m", t=PACK),
+        )
+
+        nc.vector.tensor_copy(out=a_sb[2][:], in_=a_ps[2][:])
+        nc.scalar.activation(out=boards[1][:].indirect(l2[:]), in_=a_sb[1][:], func=COPY)
+        nc.vector.tensor_copy(out=boards[0][:].indirect(l2[:]), in_=a_sb[0][:])
+        nc.scalar.activation(out=a_sb[3][:], in_=a_ps[3][:], func=COPY)
+        nc.vector.tensor_copy(out=boards[2][:].indirect(l2[:]), in_=a_sb[2][:])
+        nc.scalar.activation(out=boards[3][:].indirect(l2[:]), in_=a_sb[3][:], func=COPY)
+
+        b_ps = []
+        for h in range(2):
+            acc = psum.tile([P, PACK, HALF], F32, name="b%d" % h, tag="bank%d" % (PACK + h))
+            for t in range(PACK):
+                nc.tensor.matmul_mx(
+                    out=acc[:, t, :],
+                    lhsT=w2wp[:, P * t : P * (t + 1)].bitcast(E4M3),
+                    lhsT_scale=w2scp[:, P * t : P * (t + 1)],
+                    rhs=xg[:, HALF * h : HALF * (h + 1)].bitcast(E5M2),
+                    rhs_scale=xsg[:, HALF * h : HALF * (h + 1)],
+                    start=True,
+                    stop=True,
+                )
+            b_ps.append(acc)
+
+        p_ps = {}
+        for h in range(2):
+            for n in range(2):
+                acc = psum.tile([P, HALF], F32, name="p%d%d" % (h, n), tag="bank%d" % (2 * h + n))
+                nc.tensor.matmul_mx(
+                    out=acc[:],
+                    lhsT=wsw[:, 2 * P * n : 2 * P * (n + 1)].bitcast(E2M1),
+                    lhsT_scale=wssc[:, P * n : P * (n + 1)],
+                    rhs=xg[:, HALF * h : HALF * (h + 1)].bitcast(E5M2),
+                    rhs_scale=xsg[:, HALF * h : HALF * (h + 1)],
+                    start=True,
+                    stop=False,
+                )
+                p_ps[h, n] = acc
+
+        looked = [sb.tile([P, PACK, HALF], F32, name="looked%d" % h) for h in range(2)]
+        hid = [sb.tile([P, HALF * PACK], BF16, name="hid%d" % h, align_bytes=64) for h in range(2)]
+        hid_codes = [sb.tile([P, HALF], U32, name="hid_codes%d" % h, align_bytes=64) for h in range(2)]
+        hid_scales = [sb.tile([P, HALF], U8, name="hid_scales%d" % h, align_bytes=64) for h in range(2)]
+        p_sb = [sb.tile([P, J], F32, name="p_sb%d" % n) for n in range(2)]
+
+        def look(on_vector, h, t):
+            window = boards[t][:].indirect(l3[:, 8 * h : 8 * (h + 1)])
+            if on_vector:
+                nc.vector.tensor_copy(out=looked[h][:, t, :], in_=window)
+            else:
+                nc.scalar.activation(out=looked[h][:, t, :], in_=window, func=COPY)
+
+        def larger(h):
+            nc.vector.tensor_tensor(
+                out=hid[h][:].rearrange("p (c i t) -> p c t i", i=4, t=PACK),
+                in0=looked[h][:].rearrange("p t (c i) -> p c t i", i=4),
+                in1=b_ps[h][:].rearrange("p t (c i) -> p c t i", i=4),
+                op=MAX,
+            )
+
+        def quantise(h):
+            nc.vector.quantize_mx(out=hid_codes[h][:].bitcast(E4M3), scales=hid_scales[h][:], in_=hid[h][:])
+
+        def second_stage(h):
+            for n in range(2):
+                nc.tensor.matmul_mx(
+                    out=p_ps[h, n][:],
+                    lhsT=wbw[:, 2 * P * n : 2 * P * (n + 1)].bitcast(E2M1),
+                    lhsT_scale=wbsc[:, P * n : P * (n + 1)],
+                    rhs=hid_codes[h][:].bitcast(E4M3),
+                    rhs_scale=hid_scales[h][:],
+                    start=False,
+                    stop=True,
+                )
+
+        look(True, 0, 0)
+        look(False, 0, 1)
+        look(True, 0, 2)
+        look(False, 0, 3)
+        look(True, 1, 0)
+        larger(0)
+        look(False, 1, 1)
+        look(False, 1, 3)
+        look(False, 1, 2)
+        quantise(0)
+        second_stage(0)
+        larger(1)
+        for n in range(2):
+            nc.scalar.activation(out=p_sb[n][:, 0:HALF], in_=p_ps[0, n][:], func=COPY)
+        quantise(1)
+        second_stage(1)
+        nc.vector.tensor_copy(out=p_sb[0][:, HALF:J], in_=p_ps[1, 0][:])
+        nc.scalar.activation(out=p_sb[1][:, HALF:J], in_=p_ps[1, 1][:], func=COPY)
+
+        pair = [sb.tile([P, 2, E], F32, name="pair%d" % n) for n in range(2)]
+        for i, lst in enumerate((l4, l5)):
+            nc.vector.tensor_copy(out=pair[0][:, i, :], in_=p_sb[0][:].indirect(lst[:]))
+            nc.scalar.activation(out=pair[1][:, i, :], in_=p_sb[1][:].indirect(lst[:]), func=COPY)
+        for n in range(2):
+            best = sb.tile([P, E], F32, name="best%d" % n)
+            nc.vector.tensor_tensor(out=best[:], in0=pair[n][:, 0, :], in1=pair[n][:, 1, :], op=MAX)
+            (nc.sync, nc.scalar)[n].dma_start(out=out[P * n : P * (n + 1), :], in_=best[:])

@@ -43,40 +43,45 @@ def tile_list_twow_board_skip_bestoftwo_kernel(
                 in_=src[0, 4 * q : 4 * q + 4, :].bitcast(I32),
             )
 
+        def load_scale_quadrant(queue, plane, src, q):
+            queue.dma_start(
+                out=plane[32 * q : 32 * (q + 1), :].bitcast(I32),
+                in_=src[0, 4 * q : 4 * q + 4, :].bitcast(I32).partition_broadcast(8),
+            )
+
         def zeroed_plane(width, name):
             plane = sb.tile([P, width], U8, name=name, align_bytes=64)
             nc.vector.memset(plane[:].bitcast(I32), 0)
             return plane
 
-        def load_words(src, width, dtype, name):
+        def load_words(queue, src, width, dtype, name):
             tile = sb.tile([P, width], dtype, name=name, align_bytes=64)
-            nc.sync.dma_start(out=tile[:].bitcast(I32), in_=src.bitcast(I32))
+            queue.dma_start(out=tile[:].bitcast(I32), in_=src.bitcast(I32))
             return tile
 
-        xs = zeroed_plane(T, "xs")
-        wsc = zeroed_plane(R, "wsc")
+        xs = sb.tile([P, T], U8, align_bytes=64)
+        wsc = sb.tile([P, R], U8, align_bytes=64)
         later = zeroed_plane(R + 2 * N, "later")
         w2sc = later[:, 0:R]
         wssc = later[:, R : R + N]
         wbsc = later[:, R + N : R + 2 * N]
 
         l1 = list_tile(offs, "l1")
-        ww = load_words(w_words[0], 2 * R, U8, "ww")
-        xw = load_words(xt_words[0].rearrange("p n t -> p (n t)"), T, U32, "xw")
         for q in range(4):
-            load_scale_rows(nc.scalar, xs, xt_scales, q)
-        load_scale_rows(nc.gpsimd, wsc, w_scales, 0)
-        for q in range(1, 4):
-            load_scale_rows(nc.sync, wsc, w_scales, q)
-        w2w = load_words(w2_words[0].rearrange("p n t -> p (n t)"), R, U32, "w2w")
+            load_scale_quadrant((nc.scalar, nc.sync)[q % 2], xs, xt_scales, q)
+        xw = load_words(nc.sync, xt_words[0].rearrange("p n t -> p (n t)"), T, U32, "xw")
+        ww = load_words(nc.sync, w_words[0], 2 * R, U8, "ww")
+        w2w = load_words(nc.sync, w2_words[0].rearrange("p n t -> p (n t)"), R, U32, "w2w")
+        for q in range(4):
+            load_scale_quadrant((nc.gpsimd, nc.sync)[q // 2], wsc, w_scales, q)
         l2 = list_tile(offs2, "l2")
         for q in range(4):
             load_scale_rows(nc.sync, w2sc, w2_scales, q)
         l3 = list_tile(offs3, "l3")
-        wsw = load_words(ws_words[0], 2 * N, U8, "wsw")
+        wsw = load_words(nc.sync, ws_words[0], 2 * N, U8, "wsw")
         for q in range(4):
             load_scale_rows(nc.sync, wssc, ws_scales, q)
-        wbw = load_words(wb_words[0], 2 * N, U8, "wbw")
+        wbw = load_words(nc.sync, wb_words[0], 2 * N, U8, "wbw")
         for q in range(4):
             load_scale_rows(nc.sync, wbsc, wb_scales, q)
         l4 = list_tile(offs4, "l4")
@@ -85,11 +90,11 @@ def tile_list_twow_board_skip_bestoftwo_kernel(
         boards = []
         for t in range(PACK):
             board = sb.tile([P, C], F32, name="board%d" % t)
-            nc.gpsimd.memset(board[:], 0.0)
+            (nc.vector, nc.gpsimd)[t % 2].memset(board[:], 0.0)
             boards.append(board)
 
         wwp = sb.tile([P, 2 * R], U8, align_bytes=64)
-        nc.vector.tensor_copy(
+        nc.scalar.copy(
             out=wwp[:].bitcast(U16).rearrange("p (t m) -> p m t", t=PACK),
             in_=ww[:].bitcast(U16).rearrange("p (m t) -> p m t", t=PACK),
         )
@@ -98,13 +103,20 @@ def tile_list_twow_board_skip_bestoftwo_kernel(
         xg = sb.tile([P, J], U32, align_bytes=64)
         nc.vector.tensor_copy(out=xg[:], in_=xw[:].indirect(l1[:]))
 
-        wscp = sb.tile([P, R], U8, align_bytes=64)
+        w2wp = sb.tile([P, R], U32, tag="ww", align_bytes=64)
+        nc.scalar.copy(
+            out=w2wp[:].rearrange("p (t m) -> p m t", t=PACK),
+            in_=w2w[:].rearrange("p (m t) -> p m t", t=PACK),
+        )
+
+        wscp = sb.tile([P, R], U8, tag="xw", align_bytes=64)
+        for planes in (slice(0, 1), slice(1, 2), slice(2, PACK)):
+            nc.vector.tensor_copy(
+                out=wscp[:].rearrange("p (t m) -> p t m", t=PACK)[:, planes, :],
+                in_=wsc[:].rearrange("p (m t) -> p t m", t=PACK)[:, planes, :],
+            )
         a_ps = []
         for t in range(PACK):
-            nc.vector.tensor_copy(
-                out=wscp[:, P * t : P * (t + 1)],
-                in_=wsc[:].rearrange("p (m t) -> p t m", t=PACK)[:, t, :],
-            )
             acc = psum.tile([P, J], F32, name="a%d" % t, tag="bank%d" % t)
             nc.tensor.matmul_mx(
                 out=acc[:],
@@ -117,25 +129,21 @@ def tile_list_twow_board_skip_bestoftwo_kernel(
             )
             a_ps.append(acc)
 
-        a_sb = [sb.tile([P, J], F32, name="a_sb%d" % t) for t in range(PACK)]
-        for t in (0, 1):
-            nc.scalar.activation(out=a_sb[t][:], in_=a_ps[t][:], func=COPY)
+        a_sb = [sb.tile([P, J], F32, name="a_sb%d" % t, align_bytes=64) for t in range(PACK)]
+        for t in range(PACK):
+            if t % 2 == 0:
+                nc.vector.tensor_copy(out=a_sb[t][:], in_=a_ps[t][:])
+            else:
+                nc.scalar.activation(out=a_sb[t][:], in_=a_ps[t][:], func=COPY)
+        nc.vector.tensor_copy(out=boards[0][:].indirect(l2[:]), in_=a_sb[0][:])
+        nc.scalar.activation(out=boards[1][:].indirect(l2[:]), in_=a_sb[1][:], func=COPY)
 
-        w2wp = sb.tile([P, R], U32, align_bytes=64)
-        nc.vector.tensor_copy(
-            out=w2wp[:].rearrange("p (t m) -> p m t", t=PACK),
-            in_=w2w[:].rearrange("p (m t) -> p m t", t=PACK),
-        )
-        w2scp = sb.tile([P, R], U8, align_bytes=64)
+        w2scp = sb.tile([P, R], U8, tag="a_sb0", align_bytes=64)
         nc.vector.tensor_copy(
             out=w2scp[:].rearrange("p (t m) -> p t m", t=PACK),
             in_=w2sc.rearrange("p (m t) -> p t m", t=PACK),
         )
 
-        nc.vector.tensor_copy(out=a_sb[2][:], in_=a_ps[2][:])
-        nc.scalar.activation(out=boards[1][:].indirect(l2[:]), in_=a_sb[1][:], func=COPY)
-        nc.vector.tensor_copy(out=boards[0][:].indirect(l2[:]), in_=a_sb[0][:])
-        nc.scalar.activation(out=a_sb[3][:], in_=a_ps[3][:], func=COPY)
         nc.vector.tensor_copy(out=boards[2][:].indirect(l2[:]), in_=a_sb[2][:])
         nc.scalar.activation(out=boards[3][:].indirect(l2[:]), in_=a_sb[3][:], func=COPY)
 
@@ -205,29 +213,27 @@ def tile_list_twow_board_skip_bestoftwo_kernel(
                     stop=True,
                 )
 
-        look(True, 0, 0)
         look(False, 0, 1)
-        look(True, 0, 2)
-        look(False, 0, 3)
+        look(False, 0, 0)
         look(True, 1, 0)
-        larger(0)
+        look(False, 0, 3)
+        look(True, 0, 2)
+        look(True, 1, 2)
         look(False, 1, 1)
         look(False, 1, 3)
-        look(False, 1, 2)
-        quantise(0)
-        second_stage(0)
-        larger(1)
-        for n in range(2):
-            nc.scalar.activation(out=p_sb[n][:, 0:HALF], in_=p_ps[0, n][:], func=COPY)
-        quantise(1)
-        second_stage(1)
-        nc.vector.tensor_copy(out=p_sb[0][:, HALF:J], in_=p_ps[1, 0][:])
-        nc.scalar.activation(out=p_sb[1][:, HALF:J], in_=p_ps[1, 1][:], func=COPY)
+        for h in range(2):
+            larger(h)
+        for h in range(2):
+            quantise(h)
+            second_stage(h)
+        for h in range(2):
+            nc.vector.tensor_copy(out=p_sb[0][:, HALF * h : HALF * (h + 1)], in_=p_ps[h, 0][:])
+            nc.scalar.activation(out=p_sb[1][:, HALF * h : HALF * (h + 1)], in_=p_ps[h, 1][:], func=COPY)
 
         pair = [sb.tile([P, 2, E], F32, name="pair%d" % n) for n in range(2)]
-        for i, lst in enumerate((l4, l5)):
-            nc.vector.tensor_copy(out=pair[0][:, i, :], in_=p_sb[0][:].indirect(lst[:]))
-            nc.scalar.activation(out=pair[1][:, i, :], in_=p_sb[1][:].indirect(lst[:]), func=COPY)
+        for n in range(2):
+            nc.vector.tensor_copy(out=pair[n][:, 0, :], in_=p_sb[n][:].indirect(l4[:]))
+            nc.scalar.activation(out=pair[n][:, 1, :], in_=p_sb[n][:].indirect(l5[:]), func=COPY)
         for n in range(2):
             best = sb.tile([P, E], F32, name="best%d" % n)
             nc.vector.tensor_tensor(out=best[:], in0=pair[n][:, 0, :], in1=pair[n][:, 1, :], op=MAX)

@@ -67,9 +67,10 @@ def tile_list_twow_board_skip_bestoftwo_kernel(
         wbsc = later[:, R + N : R + 2 * N]
 
         l1 = list_tile(offs, "l1")
-        for q in range(4):
-            load_scale_quadrant((nc.scalar, nc.sync)[q % 2], xs, xt_scales, q)
+        load_scale_quadrant(nc.scalar, xs, xt_scales, 0)
         xw = load_words(nc.sync, xt_words[0].rearrange("p n t -> p (n t)"), T, U32, "xw")
+        for q in range(1, 4):
+            load_scale_quadrant(nc.scalar, xs, xt_scales, q)
         ww = load_words(nc.sync, w_words[0], 2 * R, U8, "ww")
         w2w = load_words(nc.sync, w2_words[0].rearrange("p n t -> p (n t)"), R, U32, "w2w")
         for q in range(4):
@@ -90,13 +91,13 @@ def tile_list_twow_board_skip_bestoftwo_kernel(
         boards = []
         for t in range(PACK):
             board = sb.tile([P, C], F32, name="board%d" % t)
-            (nc.vector, nc.gpsimd)[t % 2].memset(board[:], 0.0)
+            nc.gpsimd.memset(board[:], 0.0)
             boards.append(board)
 
         wwp = sb.tile([P, 2 * R], U8, align_bytes=64)
         nc.scalar.copy(
-            out=wwp[:].bitcast(U16).rearrange("p (t m) -> p m t", t=PACK),
-            in_=ww[:].bitcast(U16).rearrange("p (m t) -> p m t", t=PACK),
+            out=wwp[:].bitcast(U16).rearrange("p (t c i) -> p c t i", t=PACK, i=8),
+            in_=ww[:].bitcast(U16).rearrange("p (c i t) -> p c t i", t=PACK, i=8),
         )
         xsg = sb.tile([P, J], U8, align_bytes=64)
         nc.vector.tensor_copy(out=xsg[:], in_=xs[:].indirect(l1[:]))
@@ -105,8 +106,8 @@ def tile_list_twow_board_skip_bestoftwo_kernel(
 
         w2wp = sb.tile([P, R], U32, tag="ww", align_bytes=64)
         nc.scalar.copy(
-            out=w2wp[:].rearrange("p (t m) -> p m t", t=PACK),
-            in_=w2w[:].rearrange("p (m t) -> p m t", t=PACK),
+            out=w2wp[:].rearrange("p (t c i) -> p c t i", t=PACK, i=4),
+            in_=w2w[:].rearrange("p (c i t) -> p c t i", t=PACK, i=4),
         )
 
         wscp = sb.tile([P, R], U8, tag="xw", align_bytes=64)
@@ -192,9 +193,9 @@ def tile_list_twow_board_skip_bestoftwo_kernel(
 
         def larger(h):
             nc.vector.tensor_tensor(
-                out=hid[h][:].rearrange("p (c i t) -> p c t i", i=4, t=PACK),
-                in0=looked[h][:].rearrange("p t (c i) -> p c t i", i=4),
-                in1=b_ps[h][:].rearrange("p t (c i) -> p c t i", i=4),
+                out=hid[h][:].rearrange("p (c i t) -> p c t i", i=2, t=PACK),
+                in0=looked[h][:].rearrange("p t (c i) -> p c t i", i=2),
+                in1=b_ps[h][:].rearrange("p t (c i) -> p c t i", i=2),
                 op=MAX,
             )
 

@@ -67,14 +67,13 @@ def tile_list_twow_board_skip_bestoftwo_kernel(
         wbsc = later[:, R + N : R + 2 * N]
 
         l1 = list_tile(offs, "l1")
-        load_scale_quadrant(nc.scalar, xs, xt_scales, 0)
+        for q in range(4):
+            load_scale_quadrant((nc.scalar, nc.sync)[q % 2], xs, xt_scales, q)
         xw = load_words(nc.sync, xt_words[0].rearrange("p n t -> p (n t)"), T, U32, "xw")
-        for q in range(1, 4):
-            load_scale_quadrant(nc.scalar, xs, xt_scales, q)
         ww = load_words(nc.sync, w_words[0], 2 * R, U8, "ww")
         w2w = load_words(nc.sync, w2_words[0].rearrange("p n t -> p (n t)"), R, U32, "w2w")
         for q in range(4):
-            load_scale_quadrant((nc.gpsimd, nc.sync)[q // 2], wsc, w_scales, q)
+            load_scale_quadrant(nc.gpsimd if q == 0 else nc.sync, wsc, w_scales, q)
         l2 = list_tile(offs2, "l2")
         for q in range(4):
             load_scale_rows(nc.sync, w2sc, w2_scales, q)

from contextlib import ExitStack

import concourse.mybir as mybir

K, T, J, R, C, N, E = 512, 1024, 256, 512, 512, 256, 128
FLOPS = 2 * K * J * (R + R + N) + 2 * R * J * N

F32 = mybir.dt.float32
BF16 = mybir.dt.bfloat16
I32 = mybir.dt.int32
U32 = mybir.dt.uint32
U16 = mybir.dt.uint16
U8 = mybir.dt.uint8
E4M3 = mybir.dt.float8_e4m3fn_x4
E5M2 = mybir.dt.float8_e5m2_x4
E2M1 = mybir.dt.float4_e2m1fn_x4
COPY = mybir.ActivationFunctionType.Copy
MAX = mybir.AluOpType.max

P = 128
PACK = 4
HALF = J // 2


def tile_list_twow_board_skip_bestoftwo_kernel(
    tc, xt_words, xt_scales, w_words, w_scales, w2_words, w2_scales, wb_words, wb_scales,
    ws_words, ws_scales, offs, offs2, offs3, offs4, offs5, out,
):
    nc = tc.nc
    with ExitStack() as ctx:
        lists = ctx.enter_context(tc.tile_pool(name="lists", bufs=1))
        sb = ctx.enter_context(tc.tile_pool(name="sb", bufs=1))
        psum = ctx.enter_context(tc.psum_pool(name="psum", bufs=1))

        def list_tile(src, name):
            tile = lists.tile(list(src.shape), U16, name=name)
            nc.sync.dma_start(tile[:], src)
            return tile

        def load_scale_rows(queue, plane, src, q):
            queue.dma_start(
                out=plane[32 * q : 32 * q + 4, :].bitcast(I32),
                in_=src[0, 4 * q : 4 * q + 4, :].bitcast(I32),
            )

        def load_scale_quadrant(queue, plane, src, q):
            queue.dma_start(
                out=plane[32 * q : 32 * (q + 1), :].bitcast(I32),
                in_=src[0, 4 * q : 4 * q + 4, :].bitcast(I32).partition_broadcast(8),
            )

        def zeroed_plane(width, name):
            plane = sb.tile([P, width], U8, name=name, align_bytes=64)
            nc.vector.memset(plane[:].bitcast(I32), 0)
            return plane

        def load_words(queue, src, width, dtype, name):
            tile = sb.tile([P, width], dtype, name=name, align_bytes=64)
            queue.dma_start(out=tile[:].bitcast(I32), in_=src.bitcast(I32))
            return tile

        xs = sb.tile([P, T], U8, align_bytes=64)
        wsc = sb.tile([P, R], U8, align_bytes=64)
        later = zeroed_plane(R + 2 * N, "later")
        w2sc = later[:, 0:R]
        wssc = later[:, R : R + N]
        wbsc = later[:, R + N : R + 2 * N]

        l1 = list_tile(offs, "l1")
        for q in range(4):
            load_scale_quadrant((nc.scalar, nc.sync)[q % 2], xs, xt_scales, q)
        xw = load_words(nc.sync, xt_words[0].rearrange("p n t -> p (n t)"), T, U32, "xw")
        ww = load_words(nc.sync, w_words[0], 2 * R, U8, "ww")
        w2w = load_words(nc.sync, w2_words[0].rearrange("p n t -> p (n t)"), R, U32, "w2w")
        for q in range(4):
            load_scale_quadrant(nc.gpsimd if q == 0 else nc.sync, wsc, w_scales, q)
        l2 = list_tile(offs2, "l2")
        for q in range(4):
            load_scale_rows(nc.sync, w2sc, w2_scales, q)
        l3 = list_tile(offs3, "l3")
        wsw = load_words(nc.sync, ws_words[0], 2 * N, U8, "wsw")
        for q in range(4):
            load_scale_rows(nc.sync, wssc, ws_scales, q)
        wbw = load_words(nc.sync, wb_words[0], 2 * N, U8, "wbw")
        for q in range(4):
            load_scale_rows(nc.sync, wbsc, wb_scales, q)
        l4 = list_tile(offs4, "l4")
        l5 = list_tile(offs5, "l5")

        boards = []
        for t in range(PACK):
            board = sb.tile([P, C], F32, name="board%d" % t)
            nc.gpsimd.memset(board[:], 0.0)
            boards.append(board)

        wwp = sb.tile([P, 2 * R], U8, align_bytes=64)
        nc.scalar.copy(
            out=wwp[:].bitcast(U16).rearrange("p (t c i) -> p c t i", t=PACK, i=8),
            in_=ww[:].bitcast(U16).rearrange("p (c i t) -> p c t i", t=PACK, i=8),
        )
        xsg = sb.tile([P, J], U8, align_bytes=64)
        nc.vector.tensor_copy(out=xsg[:], in_=xs[:].indirect(l1[:]))
        xg = sb.tile([P, J], U32, align_bytes=64)
        nc.vector.tensor_copy(out=xg[:], in_=xw[:].indirect(l1[:]))

        w2wp = sb.tile([P, R], U32, tag="ww", align_bytes=64)
        nc.scalar.copy(
            out=w2wp[:].rearrange("p (t c i) -> p c t i", t=PACK, i=4),
            in_=w2w[:].rearrange("p (c i t) -> p c t i", t=PACK, i=4),
        )

        wscp = sb.tile([P, R], U8, tag="xw", align_bytes=64)
        for planes in (slice(0, 1), slice(1, 2), slice(2, PACK)):
            nc.vector.tensor_copy(
                out=wscp[:].rearrange("p (t m) -> p t m", t=PACK)[:, planes, :],
                in_=wsc[:].rearrange("p (m t) -> p t m", t=PACK)[:, planes, :],
            )
        a_ps = []
        for t in range(PACK):
            acc = psum.tile([P, J], F32, name="a%d" % t, tag="bank%d" % t)
            nc.tensor.matmul_mx(
                out=acc[:],
                lhsT=wwp[:, 2 * P * t : 2 * P * (t + 1)].bitcast(E2M1),
                lhsT_scale=wscp[:, P * t : P * (t + 1)],
                rhs=xg[:].bitcast(E5M2),
                rhs_scale=xsg[:],
                start=True,
                stop=True,
            )
            a_ps.append(acc)

        a_sb = [sb.tile([P, J], F32, name="a_sb%d" % t, align_bytes=64) for t in range(PACK)]
        for t in range(PACK):
            if t % 2 == 0:
                nc.vector.tensor_copy(out=a_sb[t][:], in_=a_ps[t][:])
            else:
                nc.scalar.activation(out=a_sb[t][:], in_=a_ps[t][:], func=COPY)
        nc.vector.tensor_copy(out=boards[0][:].indirect(l2[:]), in_=a_sb[0][:])
        nc.scalar.activation(out=boards[1][:].indirect(l2[:]), in_=a_sb[1][:], func=COPY)

        w2scp = sb.tile([P, R], U8, tag="a_sb0", align_bytes=64)
        nc.vector.tensor_copy(
            out=w2scp[:].rearrange("p (t m) -> p t m", t=PACK),
            in_=w2sc.rearrange("p (m t) -> p t m", t=PACK),
        )

        nc.vector.tensor_copy(out=boards[2][:].indirect(l2[:]), in_=a_sb[2][:])
        nc.scalar.activation(out=boards[3][:].indirect(l2[:]), in_=a_sb[3][:], func=COPY)

        b_ps = []
        for h in range(2):
            acc = psum.tile([P, PACK, HALF], F32, name="b%d" % h, tag="bank%d" % (PACK + h))
            for t in range(PACK):
                nc.tensor.matmul_mx(
                    out=acc[:, t, :],
                    lhsT=w2wp[:, P * t : P * (t + 1)].bitcast(E4M3),
                    lhsT_scale=w2scp[:, P * t : P * (t + 1)],
                    rhs=xg[:, HALF * h : HALF * (h + 1)].bitcast(E5M2),
                    rhs_scale=xsg[:, HALF * h : HALF * (h + 1)],
                    start=True,
                    stop=True,
                )
            b_ps.append(acc)

        p_ps = {}
        for h in range(2):
            for n in range(2):
                acc = psum.tile([P, HALF], F32, name="p%d%d" % (h, n), tag="bank%d" % (2 * h + n))
                nc.tensor.matmul_mx(
                    out=acc[:],
                    lhsT=wsw[:, 2 * P * n : 2 * P * (n + 1)].bitcast(E2M1),
                    lhsT_scale=wssc[:, P * n : P * (n + 1)],
                    rhs=xg[:, HALF * h : HALF * (h + 1)].bitcast(E5M2),
                    rhs_scale=xsg[:, HALF * h : HALF * (h + 1)],
                    start=True,
                    stop=False,
                )
                p_ps[h, n] = acc

        looked = [sb.tile([P, PACK, HALF], F32, name="looked%d" % h) for h in range(2)]
        hid = [sb.tile([P, HALF * PACK], BF16, name="hid%d" % h, align_bytes=64) for h in range(2)]
        hid_codes = [sb.tile([P, HALF], U32, name="hid_codes%d" % h, align_bytes=64) for h in range(2)]
        hid_scales = [sb.tile([P, HALF], U8, name="hid_scales%d" % h, align_bytes=64) for h in range(2)]
        p_sb = [sb.tile([P, J], F32, name="p_sb%d" % n) for n in range(2)]

        def look(on_vector, h, t):
            window = boards[t][:].indirect(l3[:, 8 * h : 8 * (h + 1)])
            if on_vector:
                nc.vector.tensor_copy(out=looked[h][:, t, :], in_=window)
            else:
                nc.scalar.activation(out=looked[h][:, t, :], in_=window, func=COPY)

        def larger(h):
            nc.vector.tensor_tensor(
                out=hid[h][:].rearrange("p (c i t) -> p c t i", i=2, t=PACK),
                in0=looked[h][:].rearrange("p t (c i) -> p c t i", i=2),
                in1=b_ps[h][:].rearrange("p t (c i) -> p c t i", i=2),
                op=MAX,
            )

        def quantise(h):
            nc.vector.quantize_mx(out=hid_codes[h][:].bitcast(E4M3), scales=hid_scales[h][:], in_=hid[h][:])

        def second_stage(h):
            for n in range(2):
                nc.tensor.matmul_mx(
                    out=p_ps[h, n][:],
                    lhsT=wbw[:, 2 * P * n : 2 * P * (n + 1)].bitcast(E2M1),
                    lhsT_scale=wbsc[:, P * n : P * (n + 1)],
                    rhs=hid_codes[h][:].bitcast(E4M3),
                    rhs_scale=hid_scales[h][:],
                    start=False,
                    stop=True,
                )

        look(False, 0, 1)
        look(False, 0, 0)
        look(True, 1, 0)
        look(False, 0, 3)
        look(True, 0, 2)
        look(True, 1, 2)
        look(False, 1, 1)
        look(False, 1, 3)
        for h in range(2):
            larger(h)
        for h in range(2):
            quantise(h)
            second_stage(h)
        for h in range(2):
            nc.vector.tensor_copy(out=p_sb[0][:, HALF * h : HALF * (h + 1)], in_=p_ps[h, 0][:])
            nc.scalar.activation(out=p_sb[1][:, HALF * h : HALF * (h + 1)], in_=p_ps[h, 1][:], func=COPY)

        pair = [sb.tile([P, 2, E], F32, name="pair%d" % n) for n in range(2)]
        for n in range(2):
            nc.vector.tensor_copy(out=pair[n][:, 0, :], in_=p_sb[n][:].indirect(l4[:]))
            nc.scalar.activation(out=pair[n][:, 1, :], in_=p_sb[n][:].indirect(l5[:]), func=COPY)
        for n in range(2):
            best = sb.tile([P, E], F32, name="best%d" % n)
            nc.vector.tensor_tensor(out=best[:], in0=pair[n][:, 0, :], in1=pair[n][:, 1, :], op=MAX)
            (nc.sync, nc.scalar)[n].dma_start(out=out[P * n : P * (n + 1), :], in_=best[:])
